import numpy as np
import ml_dtypes


def mxq(x, axis, fmt="e4m3"):
    dtype, down = {"e4m3": (ml_dtypes.float8_e4m3fn, 7), "e5m2": (ml_dtypes.float8_e5m2, 14)}[fmt]
    v = np.moveaxis(np.asarray(x, np.float32).astype(ml_dtypes.bfloat16).astype(np.float64), axis, -1)
    blocks = v.reshape(v.shape[:-1] + (-1, 32))
    amax = np.abs(blocks).max(-1, keepdims=True)
    byte = np.maximum(np.where(amax > 0, np.frexp(amax)[1] - 1 + 127, 0) - down, 1)
    scale = np.exp2(byte - 127.0)
    codes = (blocks / scale).astype(np.float32).astype(dtype).astype(np.float64)
    return np.moveaxis((codes * scale).reshape(v.shape), -1, axis)


WIDE = False


def mx_kscale(k):
    if not WIDE:
        return np.ones(k)
    levels = np.array([10, -10, 5, -5, 0])
    if k % 512:
        return np.exp2(np.random.permutation(np.resize(levels, k // 32))).repeat(32)
    a = np.empty((k // 512, 16))
    for p in range(k // 512):
        a[p, :8] = np.random.permutation(np.resize(levels, 8))
        for g in range(8):
            far = levels[np.abs(levels - a[p, g]) >= 10]
            a[p, g + 8] = far[np.random.randint(len(far))]
    return np.exp2(a.ravel()).repeat(32)


def f64(x):
    return np.asarray(x).astype(np.float64)


def striped(idx):
    return np.tile(idx.reshape(-1, 16).T, (8, 1)).astype(np.uint16)


def unstriped(offs):
    return offs[:16].T.reshape(-1).astype(np.int64)


def relu2(v):
    return np.maximum(v, 0.0) ** 2


K, T, D, S, V, H, N = 512, 2048, 4, 512, 256, 1024, 256


def setup_inputs():
    n = np.random.standard_normal
    s = mx_kscale(K)[:, None]
    u = mx_kscale(H)
    return {
        "xT": (n((K, T)) * s).astype(np.float32),
        "w1": (n((K, H)) / np.sqrt(K) / s * u).astype(np.float32),
        "w2": (n((H, N)) / np.sqrt(H) / u[:, None] ** 2).astype(np.float32),
        "gate": np.tile(np.random.uniform(0.2, 1.0, (D, 1, V)) / np.sqrt(D), (1, N, 1)).astype(np.float32),
        "offs": striped(np.random.permutation(T)[:S]),
        "pos1": striped(np.random.permutation(S)[:V]),
        "pos2": striped(np.random.permutation(S)[:V]),
        "pos3": striped(np.random.permutation(S)[:V]),
        "pos4": striped(np.random.permutation(S)[:V]),
    }


def reference(xT, w1, w2, gate, offs, pos1, pos2, pos3, pos4):
    idx = unstriped(offs)
    xq = mxq(f64(xT)[:, idx], 0, "e4m3")
    h = relu2(mxq(f64(w1), 0, "e4m3").T @ xq)
    y = mxq(f64(w2), 0, "e4m3").T @ mxq(h, 0, "e4m3")
    return sum(f64(gate[d]) * y[:, unstriped(p)] for d, p in enumerate((pos1, pos2, pos3, pos4)))

@@ -1,0 +1,195 @@
+from contextlib import ExitStack
+
+import concourse.mybir as mybir
+
+K, T, D, S, V, H, N = 512, 2048, 4, 512, 256, 1024, 256
+FLOPS = 2 * K * H * S + 2 * H * N * S
+
+F32 = mybir.dt.float32
+BF16 = mybir.dt.bfloat16
+U32 = mybir.dt.uint32
+U16 = mybir.dt.uint16
+U8 = mybir.dt.uint8
+FP8X4 = mybir.dt.float8_e4m3fn_x4
+ACT = mybir.ActivationFunctionType
+ALU = mybir.AluOpType
+
+P = 128
+PACK = 4
+PASS = P * PACK
+Q = 128
+RELU_ON = "SSSVSVVS"
+SQUARE_ON = "SSSSSSSV"
+
+
+def tile_picked_sub_mlp_relu2_sub_e_kernel(tc, xT, w1, w2, gate, offs, pos1, pos2, pos3, pos4, out):
+    nc = tc.nc
+    with ExitStack() as ctx:
+        keep = ctx.enter_context(tc.tile_pool(name="keep", bufs=1))
+        ring = ctx.enter_context(tc.tile_pool(name="ring", bufs=4))
+        psum = ctx.enter_context(tc.psum_pool(name="psum", bufs=4))
+
+        offs_sb = keep.tile([P, S // 16], U16, name="offs_sb")
+        pos_sb = [keep.tile([P, V // 16], U16, name=f"pos_sb{d}") for d in range(D)]
+
+        warm_in = keep.tile([P, 8], F32, name="warm_in")
+        warm_out = keep.tile([P, 8], F32, name="warm_out")
+        nc.vector.memset(warm_in[:], 0.0)
+        nc.scalar.activation(warm_out[:], warm_in[:], ACT.Square)
+
+        x_rows = xT.rearrange("(p j) t -> p j t", j=PACK)
+        x_raw = [keep.tile([P, T], F32, name=f"x_raw{j}") for j in range(PACK)]
+        w1_rows = w1.rearrange("(p j) c -> p j c", j=PACK)
+        w1_raw = [keep.tile([P, PACK, 256], F32, name=f"w1_raw{c}") for c in range(4)]
+        w2_rows = w2.rearrange("(g p j) c -> g p j c", p=P, j=PACK)
+        w2_raw = [keep.tile([P, PACK, N], F32, name=f"w2_raw{g}") for g in range(2)]
+        gate_sb = [keep.tile([P, D, V], F32, name=f"gate_sb{b}") for b in range(2)]
+
+        nc.sync.dma_start(x_raw[0][:], x_rows[:, 0, :])
+        nc.sync.dma_start(offs_sb[:], offs)
+        for j in range(1, PACK):
+            nc.sync.dma_start(x_raw[j][:], x_rows[:, j, :])
+        for c in range(4):
+            nc.sync.dma_start(w1_raw[c][:], w1_rows[:, :, 256 * c : 256 * (c + 1)])
+        for g in range(2):
+            nc.sync.dma_start(w2_raw[g][:], w2_rows[g])
+        for d, pos in enumerate((pos1, pos2, pos3, pos4)):
+            nc.sync.dma_start(pos_sb[d][:], pos)
+        for b in range(2):
+            nc.sync.dma_start(gate_sb[b][:], gate[:, P * b : P * (b + 1), :].rearrange("d p v -> p d v"))
+
+        def quantize(codes, scales, grouped):
+            nc.vector.quantize_mx(out=codes.bitcast(FP8X4), scales=scales, in_=grouped)
+
+        def copy_on(engine, dst, src):
+            if engine == "S":
+                nc.scalar.copy(dst, src)
+            else:
+                nc.vector.tensor_copy(dst, src)
+
+        x_grouped = keep.tile([P, S, PACK], BF16, name="x_grouped", align_bytes=64)
+        x_codes = keep.tile([P, S], U32, name="x_codes", align_bytes=64)
+        x_scales = keep.tile([P, S], U8, name="x_scales", align_bytes=64)
+        for j in range(PACK - 1):
+            nc.vector.tensor_copy(x_grouped[:, :, j], x_raw[j][:].indirect(offs_sb[:]))
+
+        def x_half(h):
+            n = slice(256 * h, 256 * (h + 1))
+            nc.vector.tensor_copy(x_grouped[:, n, PACK - 1], x_raw[PACK - 1][:].indirect(offs_sb[:, 16 * h : 16 * (h + 1)]))
+
+        def x_quant(h):
+            n = slice(256 * h, 256 * (h + 1))
+            quantize(x_codes[:, n], x_scales[:, n], x_grouped[:, n, :].rearrange("p n j -> p (n j)"))
+
+        w1_grouped = [keep.tile([P, PACK, P, PACK], BF16, name=f"w1_grouped{g}", align_bytes=64) for g in range(2)]
+        w1_codes = [keep.tile([P, PASS], U32, name=f"w1_codes{g}", align_bytes=64) for g in range(2)]
+        w1_scales = [keep.tile([P, PASS], U8, name=f"w1_scales{g}", align_bytes=64) for g in range(2)]
+
+        def w1_cast(c, m0, m1, engine):
+            g, half = divmod(c, 2)
+            dst = w1_grouped[g][:, :, 64 * half + m0 : 64 * half + m1, :].rearrange("p t m j -> p m j t")
+            src = w1_raw[c][:, :, PACK * m0 : PACK * m1].rearrange("p j (m t) -> p m j t", t=PACK)
+            copy_on(engine, dst, src)
+
+        def w1_quant(g):
+            for u in range(2):
+                cols = slice(256 * u, 256 * (u + 1))
+                quantize(w1_codes[g][:, cols], w1_scales[g][:, cols],
+                         w1_grouped[g][:, 2 * u : 2 * u + 2, :, :].rearrange("p t m j -> p (t m j)"))
+
+        w2_grouped = [keep.tile([P, N, PACK], BF16, name=f"w2_grouped{g}", align_bytes=64) for g in range(2)]
+        w2_codes = [keep.tile([P, N], U32, name=f"w2_codes{g}", align_bytes=64) for g in range(2)]
+        w2_scales = [keep.tile([P, N], U8, name=f"w2_scales{g}", align_bytes=64) for g in range(2)]
+
+        def w2_cast(g):
+            nc.vector.tensor_copy(
+                w2_grouped[g][:].rearrange("p (c i) j -> p c j i", i=4),
+                w2_raw[g][:].rearrange("p j (c i) -> p c j i", i=4),
+            )
+
+        def w2_quant(g):
+            quantize(w2_codes[g][:], w2_scales[g][:], w2_grouped[g][:].rearrange("p c j -> p (c j)"))
+
+        h_codes = [keep.tile([P, S], U32, name=f"h_codes{g}", align_bytes=64) for g in range(2)]
+        h_scales = [keep.tile([P, S], U8, name=f"h_scales{g}", align_bytes=64) for g in range(2)]
+        y_sb = [keep.tile([P, S], F32, name=f"y_sb{b}") for b in range(2)]
+
+        def layer1(u):
+            g, q = divmod(u, 4)
+            n = slice(Q * q, Q * (q + 1))
+            pre = psum.tile([P, PACK, Q], F32, name="pre")
+            for t in range(PACK):
+                cols = slice(P * t, P * (t + 1))
+                nc.tensor.matmul_mx(
+                    out=pre[:, t, :], lhsT=w1_codes[g][:, cols].bitcast(FP8X4), lhsT_scale=w1_scales[g][:, cols],
+                    rhs=x_codes[:, n].bitcast(FP8X4), rhs_scale=x_scales[:, n], start=True, stop=True)
+            rect = ring.tile([P, Q, PACK], F32, name="rect")
+            src = pre[:].rearrange("p t n -> p n t")
+            if RELU_ON[u] == "S":
+                nc.scalar.activation(rect[:], src, ACT.Relu)
+            else:
+                nc.vector.tensor_scalar_max(rect[:], src, 0.0)
+            h_grouped = ring.tile([P, Q * PACK], BF16, name="h_grouped", align_bytes=64)
+            flat = rect[:].rearrange("p n t -> p (n t)")
+            if SQUARE_ON[u] == "S":
+                nc.scalar.activation(h_grouped[:], flat, ACT.Square)
+            else:
+                nc.vector.tensor_tensor(h_grouped[:], flat, flat, ALU.mult)
+            quantize(h_codes[g][:, n], h_scales[g][:, n], h_grouped[:])
+
+        def layer2(q, b):
+            n = slice(Q * q, Q * (q + 1))
+            cols = slice(P * b, P * (b + 1))
+            acc = psum.tile([P, Q], F32, name="acc")
+            for g in range(2):
+                nc.tensor.matmul_mx(
+                    out=acc[:], lhsT=w2_codes[g][:, cols].bitcast(FP8X4), lhsT_scale=w2_scales[g][:, cols],
+                    rhs=h_codes[g][:, n].bitcast(FP8X4), rhs_scale=h_scales[g][:, n], start=(g == 0), stop=(g == 1))
+            nc.scalar.copy(y_sb[b][:, n], acc[:])
+
+        x_half(0)
+        x_half(1)
+        x_quant(0)
+        x_quant(1)
+        w1_cast(0, 0, 64, "S")
+        w1_cast(1, 0, 16, "S")
+        w1_cast(1, 16, 64, "V")
+        w1_quant(0)
+        w1_cast(2, 0, 32, "S")
+        w1_cast(2, 32, 64, "V")
+        w1_cast(3, 0, 64, "V")
+        w1_quant(1)
+        for u in range(5):
+            layer1(u)
+        for g in range(2):
+            w2_cast(g)
+            w2_quant(g)
+        for u in range(5, 8):
+            layer1(u)
+        for b in range(2):
+            for q in range(4):
+                layer2(q, b)
+
+        terms = [keep.tile([P, D, V], F32, name=f"terms{b}") for b in range(2)]
+
+        def fetch(b, d):
+            nc.vector.tensor_tensor(terms[b][:, d, :], y_sb[b][:].indirect(pos_sb[d][:]), gate_sb[b][:, d, :], ALU.mult)
+
+        pairs = keep.tile([P, 2, V], F32, name="pairs")
+        total0 = keep.tile([P, V], F32, name="total0")
+        two = keep.tile([P, V], F32, name="two")
+        three = keep.tile([P, V], F32, name="three")
+        total1 = keep.tile([P, V], F32, name="total1")
+        for d in range(D):
+            fetch(0, d)
+        fetch(1, 0)
+        nc.vector.tensor_tensor(pairs[:], terms[0][:, 0:2, :], terms[0][:, 2:4, :], ALU.add)
+        fetch(1, 1)
+        nc.vector.tensor_tensor(total0[:], pairs[:, 0, :], pairs[:, 1, :], ALU.add)
+        nc.sync.dma_start(out[0:P, :], total0[:])
+        fetch(1, 2)
+        nc.vector.tensor_tensor(two[:], terms[1][:, 0, :], terms[1][:, 1, :], ALU.add)
+        fetch(1, 3)
+        nc.vector.tensor_tensor(three[:], two[:], terms[1][:, 2, :], ALU.add)
+        nc.vector.tensor_tensor(total1[:], three[:], terms[1][:, 3, :], ALU.add)
+        nc.sync.dma_start(out[P : 2 * P, :], total1[:])

@@ -1,6 +1,7 @@
 from contextlib import ExitStack
 
 import concourse.mybir as mybir
+from concourse.masks import make_identity
 
 K, T, D, S, V, H, N = 512, 2048, 4, 512, 256, 1024, 256
 FLOPS = 2 * K * H * S + 2 * H * N * S
@@ -18,8 +19,9 @@ P = 128
 PACK = 4
 PASS = P * PACK
 Q = 128
-RELU_ON = "SSSVSVVS"
-SQUARE_ON = "SSSSSSSV"
+RELU_ON = "SSSSSSSV"
+SQUARE_ON = "VVSSVSSV"
+SCALAR_SHARE = (64, 16, 48, 0)
 
 
 def tile_picked_sub_mlp_relu2_sub_e_kernel(tc, xT, w1, w2, gate, offs, pos1, pos2, pos3, pos4, out):
@@ -36,6 +38,9 @@ def tile_picked_sub_mlp_relu2_sub_e_kernel(tc, xT, w1, w2, gate, offs, pos1, pos
         warm_out = keep.tile([P, 8], F32, name="warm_out")
         nc.vector.memset(warm_in[:], 0.0)
         nc.scalar.activation(warm_out[:], warm_in[:], ACT.Square)
+
+        ident = keep.tile([P, P], F32, name="ident")
+        make_identity(nc, ident[:])
 
         x_rows = xT.rearrange("(p j) t -> p j t", j=PACK)
         x_raw = [keep.tile([P, T], F32, name=f"x_raw{j}") for j in range(PACK)]
@@ -91,27 +96,35 @@ def tile_picked_sub_mlp_relu2_sub_e_kernel(tc, xT, w1, w2, gate, offs, pos1, pos
             src = w1_raw[c][:, :, PACK * m0 : PACK * m1].rearrange("p j (m t) -> p m j t", t=PACK)
             copy_on(engine, dst, src)
 
-        def w1_quant(g):
-            for u in range(2):
-                cols = slice(256 * u, 256 * (u + 1))
+        def w1_pass(g, slots):
+            for c in (2 * g, 2 * g + 1):
+                if SCALAR_SHARE[c] > 0:
+                    w1_cast(c, 0, SCALAR_SHARE[c], "S")
+                if SCALAR_SHARE[c] < 64:
+                    w1_cast(c, SCALAR_SHARE[c], 64, "V")
+            for t in range(0, PACK, slots):
+                cols = slice(P * t, P * (t + slots))
                 quantize(w1_codes[g][:, cols], w1_scales[g][:, cols],
-                         w1_grouped[g][:, 2 * u : 2 * u + 2, :, :].rearrange("p t m j -> p (t m j)"))
+                         w1_grouped[g][:, t : t + slots, :, :].rearrange("p t m j -> p (t m j)"))
 
         w2_grouped = [keep.tile([P, N, PACK], BF16, name=f"w2_grouped{g}", align_bytes=64) for g in range(2)]
         w2_codes = [keep.tile([P, N], U32, name=f"w2_codes{g}", align_bytes=64) for g in range(2)]
         w2_scales = [keep.tile([P, N], U8, name=f"w2_scales{g}", align_bytes=64) for g in range(2)]
 
-        def w2_cast(g):
+        def w2_cast(g, b):
+            cols = slice(P * b, P * (b + 1))
             nc.vector.tensor_copy(
-                w2_grouped[g][:].rearrange("p (c i) j -> p c j i", i=4),
-                w2_raw[g][:].rearrange("p j (c i) -> p c j i", i=4),
+                w2_grouped[g][:, cols, :].rearrange("p (c i) j -> p c j i", i=4),
+                w2_raw[g][:, :, cols].rearrange("p j (c i) -> p c j i", i=4),
             )
 
-        def w2_quant(g):
-            quantize(w2_codes[g][:], w2_scales[g][:], w2_grouped[g][:].rearrange("p c j -> p (c j)"))
+        def w2_quant(g, b):
+            cols = slice(P * b, P * (b + 1))
+            quantize(w2_codes[g][:, cols], w2_scales[g][:, cols], w2_grouped[g][:, cols, :].rearrange("p c j -> p (c j)"))
 
         h_codes = [keep.tile([P, S], U32, name=f"h_codes{g}", align_bytes=64) for g in range(2)]
         h_scales = [keep.tile([P, S], U8, name=f"h_scales{g}", align_bytes=64) for g in range(2)]
+        h_grouped = [keep.tile([P, S * PACK], BF16, name=f"h_grouped{g}", align_bytes=64) for g in range(2)]
         y_sb = [keep.tile([P, S], F32, name=f"y_sb{b}") for b in range(2)]
 
         def layer1(u):
@@ -129,18 +142,21 @@ def tile_picked_sub_mlp_relu2_sub_e_kernel(tc, xT, w1, w2, gate, offs, pos1, pos
                 nc.scalar.activation(rect[:], src, ACT.Relu)
             else:
                 nc.vector.tensor_scalar_max(rect[:], src, 0.0)
-            h_grouped = ring.tile([P, Q * PACK], BF16, name="h_grouped", align_bytes=64)
+            squared = h_grouped[g][:, PACK * Q * q : PACK * Q * (q + 1)]
             flat = rect[:].rearrange("p n t -> p (n t)")
             if SQUARE_ON[u] == "S":
-                nc.scalar.activation(h_grouped[:], flat, ACT.Square)
+                nc.scalar.activation(squared, flat, ACT.Square)
             else:
-                nc.vector.tensor_tensor(h_grouped[:], flat, flat, ALU.mult)
-            quantize(h_codes[g][:, n], h_scales[g][:, n], h_grouped[:])
+                nc.vector.tensor_tensor(squared, flat, flat, ALU.mult)
+            if g == 1:
+                quantize(h_codes[g][:, n], h_scales[g][:, n], squared)
+            elif q == 3:
+                quantize(h_codes[g][:], h_scales[g][:], h_grouped[g][:])
 
-        def layer2(q, b):
-            n = slice(Q * q, Q * (q + 1))
+        def layer2(b, n0, width):
+            n = slice(n0, n0 + width)
             cols = slice(P * b, P * (b + 1))
-            acc = psum.tile([P, Q], F32, name="acc")
+            acc = psum.tile([P, width], F32, name="acc")
             for g in range(2):
                 nc.tensor.matmul_mx(
                     out=acc[:], lhsT=w2_codes[g][:, cols].bitcast(FP8X4), lhsT_scale=w2_scales[g][:, cols],
@@ -151,45 +167,52 @@ def tile_picked_sub_mlp_relu2_sub_e_kernel(tc, xT, w1, w2, gate, offs, pos1, pos
         x_half(1)
         x_quant(0)
         x_quant(1)
-        w1_cast(0, 0, 64, "S")
-        w1_cast(1, 0, 16, "S")
-        w1_cast(1, 16, 64, "V")
-        w1_quant(0)
-        w1_cast(2, 0, 32, "S")
-        w1_cast(2, 32, 64, "V")
-        w1_cast(3, 0, 64, "V")
-        w1_quant(1)
-        for u in range(5):
-            layer1(u)
+        w1_pass(0, 1)
+        layer1(0)
+        w1_pass(1, 2)
         for g in range(2):
-            w2_cast(g)
-            w2_quant(g)
-        for u in range(5, 8):
+            w2_cast(g, 0)
+        for g in range(2):
+            w2_quant(g, 0)
+        for u in range(1, 8):
             layer1(u)
-        for b in range(2):
-            for q in range(4):
-                layer2(q, b)
+        for q in range(4):
+            layer2(0, Q * q, Q)
+        for g in range(2):
+            w2_cast(g, 1)
+        for g in range(2):
+            w2_quant(g, 1)
+        for q in range(4):
+            layer2(1, Q * q, Q)
 
         terms = [keep.tile([P, D, V], F32, name=f"terms{b}") for b in range(2)]
 
-        def fetch(b, d):
-            nc.vector.tensor_tensor(terms[b][:, d, :], y_sb[b][:].indirect(pos_sb[d][:]), gate_sb[b][:, d, :], ALU.mult)
+        def fetch(b, d, parts=1):
+            for h in range(parts):
+                v = slice(V // parts * h, V // parts * (h + 1))
+                places = pos_sb[d][:, V // parts // 16 * h : V // parts // 16 * (h + 1)]
+                nc.vector.tensor_tensor(terms[b][:, d, v], y_sb[b][:].indirect(places), gate_sb[b][:, d, v], ALU.mult)
 
-        pairs = keep.tile([P, 2, V], F32, name="pairs")
-        total0 = keep.tile([P, V], F32, name="total0")
-        two = keep.tile([P, V], F32, name="two")
-        three = keep.tile([P, V], F32, name="three")
-        total1 = keep.tile([P, V], F32, name="total1")
-        for d in range(D):
-            fetch(0, d)
-        fetch(1, 0)
-        nc.vector.tensor_tensor(pairs[:], terms[0][:, 0:2, :], terms[0][:, 2:4, :], ALU.add)
-        fetch(1, 1)
-        nc.vector.tensor_tensor(total0[:], pairs[:, 0, :], pairs[:, 1, :], ALU.add)
-        nc.sync.dma_start(out[0:P, :], total0[:])
-        fetch(1, 2)
-        nc.vector.tensor_tensor(two[:], terms[1][:, 0, :], terms[1][:, 1, :], ALU.add)
-        fetch(1, 3)
-        nc.vector.tensor_tensor(three[:], two[:], terms[1][:, 2, :], ALU.add)
-        nc.vector.tensor_tensor(total1[:], three[:], terms[1][:, 3, :], ALU.add)
-        nc.sync.dma_start(out[P : 2 * P, :], total1[:])
+        def sum_of_three(b):
+            back = psum.tile([P, V], F32, name="acc")
+            for h in range(2):
+                turned = psum.tile([P, P], F32, name="pre")
+                for d in range(D - 1):
+                    nc.tensor.matmul(turned[:], terms[b][:, d, P * h : P * (h + 1)], ident[:],
+                                     start=(d == 0), stop=(d == D - 2), is_transpose=True)
+                turned_sb = ring.tile([P, P], F32, name="turned_sb")
+                nc.scalar.copy(turned_sb[:], turned[:])
+                nc.tensor.transpose(back[:, P * h : P * (h + 1)], turned_sb[:], ident[:])
+            return back
+
+        partial = []
+        for b in range(2):
+            for d in range(D - 1):
+                fetch(b, d, 2 if (b, d) == (1, D - 2) else 1)
+            partial.append(sum_of_three(b))
+        for b in range(2):
+            fetch(b, D - 1)
+        for b in range(2):
+            total = ring.tile([P, V], F32, name="total")
+            nc.vector.tensor_tensor(total[:], partial[b][:], terms[b][:, D - 1, :], ALU.add)
+            nc.sync.dma_start(out[P * b : P * (b + 1), :], total[:])

@@ -21,7 +21,7 @@ PASS = P * PACK
 Q = 128
 RELU_ON = "SSSSSSSV"
 SQUARE_ON = "VVSSVSSV"
-SCALAR_SHARE = (64, 16, 48, 0)
+W1_LOADS = ((0, 512, 192), (512, 256, 192), (768, 256, 0))
 
 
 def tile_picked_sub_mlp_relu2_sub_e_kernel(tc, xT, w1, w2, gate, offs, pos1, pos2, pos3, pos4, out):
@@ -45,7 +45,7 @@ def tile_picked_sub_mlp_relu2_sub_e_kernel(tc, xT, w1, w2, gate, offs, pos1, pos
         x_rows = xT.rearrange("(p j) t -> p j t", j=PACK)
         x_raw = [keep.tile([P, T], F32, name=f"x_raw{j}") for j in range(PACK)]
         w1_rows = w1.rearrange("(p j) c -> p j c", j=PACK)
-        w1_raw = [keep.tile([P, PACK, 256], F32, name=f"w1_raw{c}") for c in range(4)]
+        w1_raw = [keep.tile([P, PACK, width], F32, name=f"w1_raw{c}") for c, (first, width, share) in enumerate(W1_LOADS)]
         w2_rows = w2.rearrange("(g p j) c -> g p j c", p=P, j=PACK)
         w2_raw = [keep.tile([P, PACK, N], F32, name=f"w2_raw{g}") for g in range(2)]
         gate_sb = [keep.tile([P, D, V], F32, name=f"gate_sb{b}") for b in range(2)]
@@ -54,8 +54,8 @@ def tile_picked_sub_mlp_relu2_sub_e_kernel(tc, xT, w1, w2, gate, offs, pos1, pos
         nc.sync.dma_start(offs_sb[:], offs)
         for j in range(1, PACK):
             nc.sync.dma_start(x_raw[j][:], x_rows[:, j, :])
-        for c in range(4):
-            nc.sync.dma_start(w1_raw[c][:], w1_rows[:, :, 256 * c : 256 * (c + 1)])
+        for c, (first, width, share) in enumerate(W1_LOADS):
+            nc.sync.dma_start(w1_raw[c][:], w1_rows[:, :, first : first + width])
         for g in range(2):
             nc.sync.dma_start(w2_raw[g][:], w2_rows[g])
         for d, pos in enumerate((pos1, pos2, pos3, pos4)):
@@ -90,18 +90,18 @@ def tile_picked_sub_mlp_relu2_sub_e_kernel(tc, xT, w1, w2, gate, offs, pos1, pos
         w1_codes = [keep.tile([P, PASS], U32, name=f"w1_codes{g}", align_bytes=64) for g in range(2)]
         w1_scales = [keep.tile([P, PASS], U8, name=f"w1_scales{g}", align_bytes=64) for g in range(2)]
 
-        def w1_cast(c, m0, m1, engine):
-            g, half = divmod(c, 2)
-            dst = w1_grouped[g][:, :, 64 * half + m0 : 64 * half + m1, :].rearrange("p t m j -> p m j t")
-            src = w1_raw[c][:, :, PACK * m0 : PACK * m1].rearrange("p j (m t) -> p m j t", t=PACK)
+        def w1_cast(c, c0, c1, engine):
+            g, first = divmod(W1_LOADS[c][0], PASS)
+            dst = w1_grouped[g][:, :, (first + c0) // PACK : (first + c1) // PACK, :].rearrange("p t m j -> p m j t")
+            src = w1_raw[c][:, :, c0:c1].rearrange("p j (m t) -> p m j t", t=PACK)
             copy_on(engine, dst, src)
 
         def w1_pass(g, slots):
-            for c in (2 * g, 2 * g + 1):
-                if SCALAR_SHARE[c] > 0:
-                    w1_cast(c, 0, SCALAR_SHARE[c], "S")
-                if SCALAR_SHARE[c] < 64:
-                    w1_cast(c, SCALAR_SHARE[c], 64, "V")
+            for c, (first, width, share) in enumerate(W1_LOADS):
+                if first // PASS == g:
+                    if share > 0:
+                        w1_cast(c, 0, share, "S")
+                    w1_cast(c, share, width, "V")
             for t in range(0, PACK, slots):
                 cols = slice(P * t, P * (t + slots))
                 quantize(w1_codes[g][:, cols], w1_scales[g][:, cols],
@@ -153,15 +153,14 @@ def tile_picked_sub_mlp_relu2_sub_e_kernel(tc, xT, w1, w2, gate, offs, pos1, pos
             elif q == 3:
                 quantize(h_codes[g][:], h_scales[g][:], h_grouped[g][:])
 
-        def layer2(b, n0, width):
-            n = slice(n0, n0 + width)
+        def layer2_pass(acc, b, q, g):
+            n = slice(Q * q, Q * (q + 1))
             cols = slice(P * b, P * (b + 1))
-            acc = psum.tile([P, width], F32, name="acc")
-            for g in range(2):
-                nc.tensor.matmul_mx(
-                    out=acc[:], lhsT=w2_codes[g][:, cols].bitcast(FP8X4), lhsT_scale=w2_scales[g][:, cols],
-                    rhs=h_codes[g][:, n].bitcast(FP8X4), rhs_scale=h_scales[g][:, n], start=(g == 0), stop=(g == 1))
-            nc.scalar.copy(y_sb[b][:, n], acc[:])
+            nc.tensor.matmul_mx(
+                out=acc[:], lhsT=w2_codes[g][:, cols].bitcast(FP8X4), lhsT_scale=w2_scales[g][:, cols],
+                rhs=h_codes[g][:, n].bitcast(FP8X4), rhs_scale=h_scales[g][:, n], start=(g == 0), stop=(g == 1))
+            if g == 1:
+                nc.scalar.copy(y_sb[b][:, n], acc[:])
 
         x_half(0)
         x_half(1)
@@ -176,14 +175,18 @@ def tile_picked_sub_mlp_relu2_sub_e_kernel(tc, xT, w1, w2, gate, offs, pos1, pos
             w2_quant(g, 0)
         for u in range(1, 8):
             layer1(u)
-        for q in range(4):
-            layer2(0, Q * q, Q)
+        accs = [psum.tile([P, Q], F32, name="acc") for q in range(4)]
+        for g in range(2):
+            for q in range(4):
+                layer2_pass(accs[q], 0, q, g)
         for g in range(2):
             w2_cast(g, 1)
         for g in range(2):
             w2_quant(g, 1)
         for q in range(4):
-            layer2(1, Q * q, Q)
+            acc = psum.tile([P, Q], F32, name="pre")
+            for g in range(2):
+                layer2_pass(acc, 1, q, g)
 
         terms = [keep.tile([P, D, V], F32, name=f"terms{b}") for b in range(2)]
 
@@ -194,9 +197,9 @@ def tile_picked_sub_mlp_relu2_sub_e_kernel(tc, xT, w1, w2, gate, offs, pos1, pos
                 nc.vector.tensor_tensor(terms[b][:, d, v], y_sb[b][:].indirect(places), gate_sb[b][:, d, v], ALU.mult)
 
         def sum_of_three(b):
-            back = psum.tile([P, V], F32, name="acc")
+            back = psum.tile([P, V], F32, name="pre")
             for h in range(2):
-                turned = psum.tile([P, P], F32, name="pre")
+                turned = psum.tile([P, P], F32, name="acc")
                 for d in range(D - 1):
                     nc.tensor.matmul(turned[:], terms[b][:, d, P * h : P * (h + 1)], ident[:],
                                      start=(d == 0), stop=(d == D - 2), is_transpose=True)

@@ -18,21 +18,29 @@ ALU = mybir.AluOpType
 P = 128
 PACK = 4
 PASS = P * PACK
-Q = 128
+PASSES = H // PASS
+HALVES = N // P
+GROUP = 16
+UNIT = 128
+QUARTERS = S // UNIT
+X_PART = S // 2
+RUN = 4
+DEPTH = 4
+
 RELU_ON = "SSSSSSSV"
 SQUARE_ON = "VVSSVSSV"
-W1_LOADS = ((0, 512, 192), (512, 256, 192), (768, 256, 0))
+W1_LOADS = ((0, 256, 256), (256, 256, 64), (512, 256, 192), (768, 256, 0))
 
 
 def tile_picked_sub_mlp_relu2_sub_e_kernel(tc, xT, w1, w2, gate, offs, pos1, pos2, pos3, pos4, out):
     nc = tc.nc
     with ExitStack() as ctx:
         keep = ctx.enter_context(tc.tile_pool(name="keep", bufs=1))
-        ring = ctx.enter_context(tc.tile_pool(name="ring", bufs=4))
-        psum = ctx.enter_context(tc.psum_pool(name="psum", bufs=4))
+        ring = ctx.enter_context(tc.tile_pool(name="ring", bufs=DEPTH))
+        psum = ctx.enter_context(tc.psum_pool(name="psum", bufs=DEPTH))
 
-        offs_sb = keep.tile([P, S // 16], U16, name="offs_sb")
-        pos_sb = [keep.tile([P, V // 16], U16, name=f"pos_sb{d}") for d in range(D)]
+        offs_sb = keep.tile([P, S // GROUP], U16, name="offs_sb")
+        pos_sb = [keep.tile([P, V // GROUP], U16, name=f"pos_sb{d}") for d in range(D)]
 
         warm_in = keep.tile([P, 8], F32, name="warm_in")
         warm_out = keep.tile([P, 8], F32, name="warm_out")
@@ -47,8 +55,8 @@ def tile_picked_sub_mlp_relu2_sub_e_kernel(tc, xT, w1, w2, gate, offs, pos1, pos
         w1_rows = w1.rearrange("(p j) c -> p j c", j=PACK)
         w1_raw = [keep.tile([P, PACK, width], F32, name=f"w1_raw{c}") for c, (first, width, share) in enumerate(W1_LOADS)]
         w2_rows = w2.rearrange("(g p j) c -> g p j c", p=P, j=PACK)
-        w2_raw = [keep.tile([P, PACK, N], F32, name=f"w2_raw{g}") for g in range(2)]
-        gate_sb = [keep.tile([P, D, V], F32, name=f"gate_sb{b}") for b in range(2)]
+        w2_raw = [keep.tile([P, PACK, N], F32, name=f"w2_raw{g}") for g in range(PASSES)]
+        gate_sb = [keep.tile([P, D, V], F32, name=f"gate_sb{b}") for b in range(HALVES)]
 
         nc.sync.dma_start(x_raw[0][:], x_rows[:, 0, :])
         nc.sync.dma_start(offs_sb[:], offs)
@@ -56,11 +64,11 @@ def tile_picked_sub_mlp_relu2_sub_e_kernel(tc, xT, w1, w2, gate, offs, pos1, pos
             nc.sync.dma_start(x_raw[j][:], x_rows[:, j, :])
         for c, (first, width, share) in enumerate(W1_LOADS):
             nc.sync.dma_start(w1_raw[c][:], w1_rows[:, :, first : first + width])
-        for g in range(2):
+        for g in range(PASSES):
             nc.sync.dma_start(w2_raw[g][:], w2_rows[g])
         for d, pos in enumerate((pos1, pos2, pos3, pos4)):
             nc.sync.dma_start(pos_sb[d][:], pos)
-        for b in range(2):
+        for b in range(HALVES):
             nc.sync.dma_start(gate_sb[b][:], gate[:, P * b : P * (b + 1), :].rearrange("d p v -> p d v"))
 
         def quantize(codes, scales, grouped):
@@ -75,22 +83,23 @@ def tile_picked_sub_mlp_relu2_sub_e_kernel(tc, xT, w1, w2, gate, offs, pos1, pos
         x_grouped = keep.tile([P, S, PACK], BF16, name="x_grouped", align_bytes=64)
         x_codes = keep.tile([P, S], U32, name="x_codes", align_bytes=64)
         x_scales = keep.tile([P, S], U8, name="x_scales", align_bytes=64)
-        for j in range(PACK - 1):
-            nc.vector.tensor_copy(x_grouped[:, :, j], x_raw[j][:].indirect(offs_sb[:]))
 
-        def x_half(h):
-            n = slice(256 * h, 256 * (h + 1))
-            nc.vector.tensor_copy(x_grouped[:, n, PACK - 1], x_raw[PACK - 1][:].indirect(offs_sb[:, 16 * h : 16 * (h + 1)]))
+        def x_gather(j, first, count):
+            places = offs_sb[:, first // GROUP : (first + count) // GROUP]
+            nc.vector.tensor_copy(x_grouped[:, first : first + count, j], x_raw[j][:].indirect(places))
 
-        def x_quant(h):
-            n = slice(256 * h, 256 * (h + 1))
+        def x_quantize(first):
+            n = slice(first, first + X_PART)
             quantize(x_codes[:, n], x_scales[:, n], x_grouped[:, n, :].rearrange("p n j -> p (n j)"))
 
-        w1_grouped = [keep.tile([P, PACK, P, PACK], BF16, name=f"w1_grouped{g}", align_bytes=64) for g in range(2)]
-        w1_codes = [keep.tile([P, PASS], U32, name=f"w1_codes{g}", align_bytes=64) for g in range(2)]
-        w1_scales = [keep.tile([P, PASS], U8, name=f"w1_scales{g}", align_bytes=64) for g in range(2)]
+        for j in range(PACK - 1):
+            x_gather(j, 0, S)
 
-        def w1_cast(c, c0, c1, engine):
+        w1_grouped = [keep.tile([P, PACK, P, PACK], BF16, name=f"w1_grouped{g}", align_bytes=64) for g in range(PASSES)]
+        w1_codes = [keep.tile([P, PASS], U32, name=f"w1_codes{g}", align_bytes=64) for g in range(PASSES)]
+        w1_scales = [keep.tile([P, PASS], U8, name=f"w1_scales{g}", align_bytes=64) for g in range(PASSES)]
+
+        def w1_round(c, c0, c1, engine):
             g, first = divmod(W1_LOADS[c][0], PASS)
             dst = w1_grouped[g][:, :, (first + c0) // PACK : (first + c1) // PACK, :].rearrange("p t m j -> p m j t")
             src = w1_raw[c][:, :, c0:c1].rearrange("p j (m t) -> p m j t", t=PACK)
@@ -100,122 +109,128 @@ def tile_picked_sub_mlp_relu2_sub_e_kernel(tc, xT, w1, w2, gate, offs, pos1, pos
             for c, (first, width, share) in enumerate(W1_LOADS):
                 if first // PASS == g:
                     if share > 0:
-                        w1_cast(c, 0, share, "S")
-                    w1_cast(c, share, width, "V")
+                        w1_round(c, 0, share, "S")
+                    if share < width:
+                        w1_round(c, share, width, "V")
             for t in range(0, PACK, slots):
                 cols = slice(P * t, P * (t + slots))
                 quantize(w1_codes[g][:, cols], w1_scales[g][:, cols],
                          w1_grouped[g][:, t : t + slots, :, :].rearrange("p t m j -> p (t m j)"))
 
-        w2_grouped = [keep.tile([P, N, PACK], BF16, name=f"w2_grouped{g}", align_bytes=64) for g in range(2)]
-        w2_codes = [keep.tile([P, N], U32, name=f"w2_codes{g}", align_bytes=64) for g in range(2)]
-        w2_scales = [keep.tile([P, N], U8, name=f"w2_scales{g}", align_bytes=64) for g in range(2)]
+        w2_grouped = [keep.tile([P, N, PACK], BF16, name=f"w2_grouped{g}", align_bytes=64) for g in range(PASSES)]
+        w2_codes = [keep.tile([P, N], U32, name=f"w2_codes{g}", align_bytes=64) for g in range(PASSES)]
+        w2_scales = [keep.tile([P, N], U8, name=f"w2_scales{g}", align_bytes=64) for g in range(PASSES)]
 
-        def w2_cast(g, b):
+        def w2_half(b, engines):
             cols = slice(P * b, P * (b + 1))
-            nc.vector.tensor_copy(
-                w2_grouped[g][:, cols, :].rearrange("p (c i) j -> p c j i", i=4),
-                w2_raw[g][:, :, cols].rearrange("p j (c i) -> p c j i", i=4),
-            )
+            for g in range(PASSES):
+                copy_on(
+                    engines[g],
+                    w2_grouped[g][:, cols, :].rearrange("p (c r) j -> p c j r", r=RUN),
+                    w2_raw[g][:, :, cols].rearrange("p j (c r) -> p c j r", r=RUN),
+                )
+            for g in range(PASSES):
+                quantize(w2_codes[g][:, cols], w2_scales[g][:, cols], w2_grouped[g][:, cols, :].rearrange("p c j -> p (c j)"))
 
-        def w2_quant(g, b):
-            cols = slice(P * b, P * (b + 1))
-            quantize(w2_codes[g][:, cols], w2_scales[g][:, cols], w2_grouped[g][:, cols, :].rearrange("p c j -> p (c j)"))
-
-        h_codes = [keep.tile([P, S], U32, name=f"h_codes{g}", align_bytes=64) for g in range(2)]
-        h_scales = [keep.tile([P, S], U8, name=f"h_scales{g}", align_bytes=64) for g in range(2)]
-        h_grouped = [keep.tile([P, S * PACK], BF16, name=f"h_grouped{g}", align_bytes=64) for g in range(2)]
-        y_sb = [keep.tile([P, S], F32, name=f"y_sb{b}") for b in range(2)]
+        h_codes = [keep.tile([P, S], U32, name=f"h_codes{g}", align_bytes=64) for g in range(PASSES)]
+        h_scales = [keep.tile([P, S], U8, name=f"h_scales{g}", align_bytes=64) for g in range(PASSES)]
+        h_grouped = [keep.tile([P, S * PACK], BF16, name=f"h_grouped{g}", align_bytes=64) for g in range(PASSES)]
+        y_sb = [keep.tile([P, S], F32, name=f"y_sb{b}") for b in range(HALVES)]
 
         def layer1(u):
-            g, q = divmod(u, 4)
-            n = slice(Q * q, Q * (q + 1))
-            pre = psum.tile([P, PACK, Q], F32, name="pre")
+            g, q = divmod(u, QUARTERS)
+            n = slice(UNIT * q, UNIT * (q + 1))
+            pre = psum.tile([P, PACK, UNIT], F32, name="banks_a")
             for t in range(PACK):
                 cols = slice(P * t, P * (t + 1))
                 nc.tensor.matmul_mx(
                     out=pre[:, t, :], lhsT=w1_codes[g][:, cols].bitcast(FP8X4), lhsT_scale=w1_scales[g][:, cols],
                     rhs=x_codes[:, n].bitcast(FP8X4), rhs_scale=x_scales[:, n], start=True, stop=True)
-            rect = ring.tile([P, Q, PACK], F32, name="rect")
-            src = pre[:].rearrange("p t n -> p n t")
+            rect = ring.tile([P, UNIT, PACK], F32, name="rect")
+            by_entry = pre[:].rearrange("p t n -> p n t")
             if RELU_ON[u] == "S":
-                nc.scalar.activation(rect[:], src, ACT.Relu)
+                nc.scalar.activation(rect[:], by_entry, ACT.Relu)
             else:
-                nc.vector.tensor_scalar_max(rect[:], src, 0.0)
-            squared = h_grouped[g][:, PACK * Q * q : PACK * Q * (q + 1)]
+                nc.vector.tensor_scalar_max(rect[:], by_entry, 0.0)
+            squared = h_grouped[g][:, PACK * UNIT * q : PACK * UNIT * (q + 1)]
             flat = rect[:].rearrange("p n t -> p (n t)")
             if SQUARE_ON[u] == "S":
                 nc.scalar.activation(squared, flat, ACT.Square)
             else:
                 nc.vector.tensor_tensor(squared, flat, flat, ALU.mult)
-            if g == 1:
+            if g == PASSES - 1:
                 quantize(h_codes[g][:, n], h_scales[g][:, n], squared)
-            elif q == 3:
+            elif q == QUARTERS - 1:
                 quantize(h_codes[g][:], h_scales[g][:], h_grouped[g][:])
 
         def layer2_pass(acc, b, q, g):
-            n = slice(Q * q, Q * (q + 1))
+            n = slice(UNIT * q, UNIT * (q + 1))
             cols = slice(P * b, P * (b + 1))
             nc.tensor.matmul_mx(
                 out=acc[:], lhsT=w2_codes[g][:, cols].bitcast(FP8X4), lhsT_scale=w2_scales[g][:, cols],
-                rhs=h_codes[g][:, n].bitcast(FP8X4), rhs_scale=h_scales[g][:, n], start=(g == 0), stop=(g == 1))
-            if g == 1:
+                rhs=h_codes[g][:, n].bitcast(FP8X4), rhs_scale=h_scales[g][:, n], start=(g == 0), stop=(g == PASSES - 1))
+            if g == PASSES - 1:
                 nc.scalar.copy(y_sb[b][:, n], acc[:])
 
-        x_half(0)
-        x_half(1)
-        x_quant(0)
-        x_quant(1)
+        for first in range(0, S, X_PART):
+            x_gather(PACK - 1, first, X_PART)
+        for first in range(0, S, X_PART):
+            x_quantize(first)
         w1_pass(0, 1)
-        layer1(0)
         w1_pass(1, 2)
-        for g in range(2):
-            w2_cast(g, 0)
-        for g in range(2):
-            w2_quant(g, 0)
-        for u in range(1, 8):
+        layer1(0)
+        layer1(1)
+        w2_half(0, "VV")
+        for u in range(2, PASSES * QUARTERS):
             layer1(u)
-        accs = [psum.tile([P, Q], F32, name="acc") for q in range(4)]
-        for g in range(2):
-            for q in range(4):
+
+        accs = [psum.tile([P, UNIT], F32, name="banks_b") for q in range(QUARTERS)]
+        for g in range(PASSES):
+            for q in range(QUARTERS):
                 layer2_pass(accs[q], 0, q, g)
-        for g in range(2):
-            w2_cast(g, 1)
-        for g in range(2):
-            w2_quant(g, 1)
-        for q in range(4):
-            acc = psum.tile([P, Q], F32, name="pre")
-            for g in range(2):
+
+        w2_half(1, "SV")
+        for q in range(QUARTERS):
+            acc = psum.tile([P, UNIT], F32, name="banks_a")
+            for g in range(PASSES):
                 layer2_pass(acc, 1, q, g)
 
-        terms = [keep.tile([P, D, V], F32, name=f"terms{b}") for b in range(2)]
+        terms = [keep.tile([P, D, V], F32, name=f"terms{b}") for b in range(HALVES)]
 
-        def fetch(b, d, parts=1):
-            for h in range(parts):
-                v = slice(V // parts * h, V // parts * (h + 1))
-                places = pos_sb[d][:, V // parts // 16 * h : V // parts // 16 * (h + 1)]
+        def fetch(b, d, width):
+            for first in range(0, V, width):
+                v = slice(first, first + width)
+                places = pos_sb[d][:, first // GROUP : (first + width) // GROUP]
                 nc.vector.tensor_tensor(terms[b][:, d, v], y_sb[b][:].indirect(places), gate_sb[b][:, d, v], ALU.mult)
 
-        def sum_of_three(b):
-            back = psum.tile([P, V], F32, name="pre")
-            for h in range(2):
-                turned = psum.tile([P, P], F32, name="acc")
+        def sum_of_three(b, width):
+            sums = []
+            for first in range(0, V, P):
+                v = slice(first, first + P)
+                turned = psum.tile([P, P], F32, name="banks_b")
                 for d in range(D - 1):
-                    nc.tensor.matmul(turned[:], terms[b][:, d, P * h : P * (h + 1)], ident[:],
+                    nc.tensor.matmul(turned[:], terms[b][:, d, v], ident[:],
                                      start=(d == 0), stop=(d == D - 2), is_transpose=True)
                 turned_sb = ring.tile([P, P], F32, name="turned_sb")
                 nc.scalar.copy(turned_sb[:], turned[:])
-                nc.tensor.transpose(back[:, P * h : P * (h + 1)], turned_sb[:], ident[:])
-            return back
+                if first % width == 0:
+                    back = psum.tile([P, V], F32, name="banks_a")
+                    sums.append((first, back))
+                nc.tensor.transpose(back[:, v], turned_sb[:], ident[:])
+            return sums
 
+        widths = (V, P)
         partial = []
-        for b in range(2):
-            for d in range(D - 1):
-                fetch(b, d, 2 if (b, d) == (1, D - 2) else 1)
-            partial.append(sum_of_three(b))
-        for b in range(2):
-            fetch(b, D - 1)
-        for b in range(2):
+        for b in range(HALVES):
+            for d in range(D - 2):
+                fetch(b, d, V)
+            fetch(b, D - 2, widths[b])
+            partial.append(sum_of_three(b, widths[b]))
+        for b in range(HALVES):
+            fetch(b, D - 1, V)
+        for b in range(HALVES):
             total = ring.tile([P, V], F32, name="total")
-            nc.vector.tensor_tensor(total[:], partial[b][:], terms[b][:, D - 1, :], ALU.add)
+            for first, back in partial[b]:
+                v = slice(first, first + widths[b])
+                nc.vector.tensor_tensor(total[:, v], back[:, v], terms[b][:, D - 1, v], ALU.add)
             nc.sync.dma_start(out[P * b : P * (b + 1), :], total[:])

from contextlib import ExitStack

import concourse.mybir as mybir
from concourse.masks import make_identity

K, T, D, S, V, H, N = 512, 2048, 4, 512, 256, 1024, 256
FLOPS = 2 * K * H * S + 2 * H * N * S

F32 = mybir.dt.float32
BF16 = mybir.dt.bfloat16
U32 = mybir.dt.uint32
U16 = mybir.dt.uint16
U8 = mybir.dt.uint8
FP8X4 = mybir.dt.float8_e4m3fn_x4
ACT = mybir.ActivationFunctionType
ALU = mybir.AluOpType

P = 128
PACK = 4
PASS = P * PACK
PASSES = H // PASS
HALVES = N // P
GROUP = 16
UNIT = 128
QUARTERS = S // UNIT
X_PART = S // 2
RUN = 4
DEPTH = 4

RELU_ON = "SSSSSSSV"
SQUARE_ON = "VVSSVSSV"
W1_LOADS = ((0, 256, 256), (256, 256, 64), (512, 256, 192), (768, 256, 0))


def tile_picked_sub_mlp_relu2_sub_e_kernel(tc, xT, w1, w2, gate, offs, pos1, pos2, pos3, pos4, out):
    nc = tc.nc
    with ExitStack() as ctx:
        keep = ctx.enter_context(tc.tile_pool(name="keep", bufs=1))
        ring = ctx.enter_context(tc.tile_pool(name="ring", bufs=DEPTH))
        psum = ctx.enter_context(tc.psum_pool(name="psum", bufs=DEPTH))

        offs_sb = keep.tile([P, S // GROUP], U16, name="offs_sb")
        pos_sb = [keep.tile([P, V // GROUP], U16, name=f"pos_sb{d}") for d in range(D)]

        warm_in = keep.tile([P, 8], F32, name="warm_in")
        warm_out = keep.tile([P, 8], F32, name="warm_out")
        nc.vector.memset(warm_in[:], 0.0)
        nc.scalar.activation(warm_out[:], warm_in[:], ACT.Square)

        ident = keep.tile([P, P], F32, name="ident")
        make_identity(nc, ident[:])

        x_rows = xT.rearrange("(p j) t -> p j t", j=PACK)
        x_raw = [keep.tile([P, T], F32, name=f"x_raw{j}") for j in range(PACK)]
        w1_rows = w1.rearrange("(p j) c -> p j c", j=PACK)
        w1_raw = [keep.tile([P, PACK, width], F32, name=f"w1_raw{c}") for c, (first, width, share) in enumerate(W1_LOADS)]
        w2_rows = w2.rearrange("(g p j) c -> g p j c", p=P, j=PACK)
        w2_raw = [keep.tile([P, PACK, N], F32, name=f"w2_raw{g}") for g in range(PASSES)]
        gate_sb = [keep.tile([P, D, V], F32, name=f"gate_sb{b}") for b in range(HALVES)]

        nc.sync.dma_start(x_raw[0][:], x_rows[:, 0, :])
        nc.sync.dma_start(offs_sb[:], offs)
        for j in range(1, PACK):
            nc.sync.dma_start(x_raw[j][:], x_rows[:, j, :])
        for c, (first, width, share) in enumerate(W1_LOADS):
            nc.sync.dma_start(w1_raw[c][:], w1_rows[:, :, first : first + width])
        for g in range(PASSES):
            nc.sync.dma_start(w2_raw[g][:], w2_rows[g])
        for d, pos in enumerate((pos1, pos2, pos3, pos4)):
            nc.sync.dma_start(pos_sb[d][:], pos)
        for b in range(HALVES):
            nc.sync.dma_start(gate_sb[b][:], gate[:, P * b : P * (b + 1), :].rearrange("d p v -> p d v"))

        def quantize(codes, scales, grouped):
            nc.vector.quantize_mx(out=codes.bitcast(FP8X4), scales=scales, in_=grouped)

        def copy_on(engine, dst, src):
            if engine == "S":
                nc.scalar.copy(dst, src)
            else:
                nc.vector.tensor_copy(dst, src)

        x_grouped = keep.tile([P, S, PACK], BF16, name="x_grouped", align_bytes=64)
        x_codes = keep.tile([P, S], U32, name="x_codes", align_bytes=64)
        x_scales = keep.tile([P, S], U8, name="x_scales", align_bytes=64)

        def x_gather(j, first, count):
            places = offs_sb[:, first // GROUP : (first + count) // GROUP]
            nc.vector.tensor_copy(x_grouped[:, first : first + count, j], x_raw[j][:].indirect(places))

        def x_quantize(first):
            n = slice(first, first + X_PART)
            quantize(x_codes[:, n], x_scales[:, n], x_grouped[:, n, :].rearrange("p n j -> p (n j)"))

        for j in range(PACK - 1):
            x_gather(j, 0, S)

        w1_grouped = [keep.tile([P, PACK, P, PACK], BF16, name=f"w1_grouped{g}", align_bytes=64) for g in range(PASSES)]
        w1_codes = [keep.tile([P, PASS], U32, name=f"w1_codes{g}", align_bytes=64) for g in range(PASSES)]
        w1_scales = [keep.tile([P, PASS], U8, name=f"w1_scales{g}", align_bytes=64) for g in range(PASSES)]

        def w1_round(c, c0, c1, engine):
            g, first = divmod(W1_LOADS[c][0], PASS)
            dst = w1_grouped[g][:, :, (first + c0) // PACK : (first + c1) // PACK, :].rearrange("p t m j -> p m j t")
            src = w1_raw[c][:, :, c0:c1].rearrange("p j (m t) -> p m j t", t=PACK)
            copy_on(engine, dst, src)

        def w1_pass(g, slots):
            for c, (first, width, share) in enumerate(W1_LOADS):
                if first // PASS == g:
                    if share > 0:
                        w1_round(c, 0, share, "S")
                    if share < width:
                        w1_round(c, share, width, "V")
            for t in range(0, PACK, slots):
                cols = slice(P * t, P * (t + slots))
                quantize(w1_codes[g][:, cols], w1_scales[g][:, cols],
                         w1_grouped[g][:, t : t + slots, :, :].rearrange("p t m j -> p (t m j)"))

        w2_grouped = [keep.tile([P, N, PACK], BF16, name=f"w2_grouped{g}", align_bytes=64) for g in range(PASSES)]
        w2_codes = [keep.tile([P, N], U32, name=f"w2_codes{g}", align_bytes=64) for g in range(PASSES)]
        w2_scales = [keep.tile([P, N], U8, name=f"w2_scales{g}", align_bytes=64) for g in range(PASSES)]

        def w2_half(b, engines):
            cols = slice(P * b, P * (b + 1))
            for g in range(PASSES):
                copy_on(
                    engines[g],
                    w2_grouped[g][:, cols, :].rearrange("p (c r) j -> p c j r", r=RUN),
                    w2_raw[g][:, :, cols].rearrange("p j (c r) -> p c j r", r=RUN),
                )
            for g in range(PASSES):
                quantize(w2_codes[g][:, cols], w2_scales[g][:, cols], w2_grouped[g][:, cols, :].rearrange("p c j -> p (c j)"))

        h_codes = [keep.tile([P, S], U32, name=f"h_codes{g}", align_bytes=64) for g in range(PASSES)]
        h_scales = [keep.tile([P, S], U8, name=f"h_scales{g}", align_bytes=64) for g in range(PASSES)]
        h_grouped = [keep.tile([P, S * PACK], BF16, name=f"h_grouped{g}", align_bytes=64) for g in range(PASSES)]
        y_sb = [keep.tile([P, S], F32, name=f"y_sb{b}") for b in range(HALVES)]

        def layer1(u):
            g, q = divmod(u, QUARTERS)
            n = slice(UNIT * q, UNIT * (q + 1))
            pre = psum.tile([P, PACK, UNIT], F32, name="banks_a")
            for t in range(PACK):
                cols = slice(P * t, P * (t + 1))
                nc.tensor.matmul_mx(
                    out=pre[:, t, :], lhsT=w1_codes[g][:, cols].bitcast(FP8X4), lhsT_scale=w1_scales[g][:, cols],
                    rhs=x_codes[:, n].bitcast(FP8X4), rhs_scale=x_scales[:, n], start=True, stop=True)
            rect = ring.tile([P, UNIT, PACK], F32, name="rect")
            by_entry = pre[:].rearrange("p t n -> p n t")
            if RELU_ON[u] == "S":
                nc.scalar.activation(rect[:], by_entry, ACT.Relu)
            else:
                nc.vector.tensor_scalar_max(rect[:], by_entry, 0.0)
            squared = h_grouped[g][:, PACK * UNIT * q : PACK * UNIT * (q + 1)]
            flat = rect[:].rearrange("p n t -> p (n t)")
            if SQUARE_ON[u] == "S":
                nc.scalar.activation(squared, flat, ACT.Square)
            else:
                nc.vector.tensor_tensor(squared, flat, flat, ALU.mult)
            if g == PASSES - 1:
                quantize(h_codes[g][:, n], h_scales[g][:, n], squared)
            elif q == QUARTERS - 1:
                quantize(h_codes[g][:], h_scales[g][:], h_grouped[g][:])

        def layer2_pass(acc, b, q, g):
            n = slice(UNIT * q, UNIT * (q + 1))
            cols = slice(P * b, P * (b + 1))
            nc.tensor.matmul_mx(
                out=acc[:], lhsT=w2_codes[g][:, cols].bitcast(FP8X4), lhsT_scale=w2_scales[g][:, cols],
                rhs=h_codes[g][:, n].bitcast(FP8X4), rhs_scale=h_scales[g][:, n], start=(g == 0), stop=(g == PASSES - 1))
            if g == PASSES - 1:
                nc.scalar.copy(y_sb[b][:, n], acc[:])

        for first in range(0, S, X_PART):
            x_gather(PACK - 1, first, X_PART)
        for first in range(0, S, X_PART):
            x_quantize(first)
        w1_pass(0, 1)
        w1_pass(1, 2)
        layer1(0)
        layer1(1)
        w2_half(0, "VV")
        for u in range(2, PASSES * QUARTERS):
            layer1(u)

        accs = [psum.tile([P, UNIT], F32, name="banks_b") for q in range(QUARTERS)]
        for g in range(PASSES):
            for q in range(QUARTERS):
                layer2_pass(accs[q], 0, q, g)

        w2_half(1, "SV")
        for q in range(QUARTERS):
            acc = psum.tile([P, UNIT], F32, name="banks_a")
            for g in range(PASSES):
                layer2_pass(acc, 1, q, g)

        terms = [keep.tile([P, D, V], F32, name=f"terms{b}") for b in range(HALVES)]

        def fetch(b, d, width):
            for first in range(0, V, width):
                v = slice(first, first + width)
                places = pos_sb[d][:, first // GROUP : (first + width) // GROUP]
                nc.vector.tensor_tensor(terms[b][:, d, v], y_sb[b][:].indirect(places), gate_sb[b][:, d, v], ALU.mult)

        def sum_of_three(b, width):
            sums = []
            for first in range(0, V, P):
                v = slice(first, first + P)
                turned = psum.tile([P, P], F32, name="banks_b")
                for d in range(D - 1):
                    nc.tensor.matmul(turned[:], terms[b][:, d, v], ident[:],
                                     start=(d == 0), stop=(d == D - 2), is_transpose=True)
                turned_sb = ring.tile([P, P], F32, name="turned_sb")
                nc.scalar.copy(turned_sb[:], turned[:])
                if first % width == 0:
                    back = psum.tile([P, V], F32, name="banks_a")
                    sums.append((first, back))
                nc.tensor.transpose(back[:, v], turned_sb[:], ident[:])
            return sums

        widths = (V, P)
        partial = []
        for b in range(HALVES):
            for d in range(D - 2):
                fetch(b, d, V)
            fetch(b, D - 2, widths[b])
            partial.append(sum_of_three(b, widths[b]))
        for b in range(HALVES):
            fetch(b, D - 1, V)
        for b in range(HALVES):
            total = ring.tile([P, V], F32, name="total")
            for first, back in partial[b]:
                v = slice(first, first + widths[b])
                nc.vector.tensor_tensor(total[:, v], back[:, v], terms[b][:, D - 1, v], ALU.add)
            nc.sync.dma_start(out[P * b : P * (b + 1), :], total[:])
